import numpy as np
import ml_dtypes


def mxq(x, axis, fmt="e4m3"):
    dtype, down = {"e4m3": (ml_dtypes.float8_e4m3fn, 7), "e5m2": (ml_dtypes.float8_e5m2, 14)}[fmt]
    v = np.moveaxis(np.asarray(x, np.float32).astype(ml_dtypes.bfloat16).astype(np.float64), axis, -1)
    blocks = v.reshape(v.shape[:-1] + (-1, 32))
    amax = np.abs(blocks).max(-1, keepdims=True)
    byte = np.maximum(np.where(amax > 0, np.frexp(amax)[1] - 1 + 127, 0) - down, 1)
    scale = np.exp2(byte - 127.0)
    codes = (blocks / scale).astype(np.float32).astype(dtype).astype(np.float64)
    return np.moveaxis((codes * scale).reshape(v.shape), -1, axis)


WIDE = False


def mx_kscale(k):
    if not WIDE:
        return np.ones(k)
    levels = np.array([10, -10, 5, -5, 0])
    if k % 512:
        return np.exp2(np.random.permutation(np.resize(levels, k // 32))).repeat(32)
    a = np.empty((k // 512, 16))
    for p in range(k // 512):
        a[p, :8] = np.random.permutation(np.resize(levels, 8))
        for g in range(8):
            far = levels[np.abs(levels - a[p, g]) >= 10]
            a[p, g + 8] = far[np.random.randint(len(far))]
    return np.exp2(a.ravel()).repeat(32)


def f64(x):
    return np.asarray(x).astype(np.float64)


def striped(idx):
    return np.tile(idx.reshape(-1, 16).T, (8, 1)).astype(np.uint16)


def unstriped(offs):
    return offs[:16].T.reshape(-1).astype(np.int64)


def striped8(idx):
    return np.concatenate([x.reshape(-1, 16).T for x in idx]).astype(np.uint16)


def runs(offs, k):
    lists = np.stack([offs[16 * r : 16 * r + 16].T.reshape(-1) for r in range(8)]).astype(np.int64)
    return lists[np.arange(k) % 512 // 64]


def pack_weight(w):
    k, n = w.shape
    w = f64(np.asarray(w, np.float32).astype(ml_dtypes.bfloat16)).reshape(k // 32, 32, n)
    amax = np.abs(w).max(1)
    byte = np.clip(np.where(amax > 0, np.frexp(amax)[1] - 1 + 127 - 7, 1), 1, 254)
    scaled = (w * np.exp2(127.0 - byte)[:, None, :]).reshape(k, n).astype(np.float32)
    words = np.ascontiguousarray(scaled.reshape(k // 512, 128, 4, n).transpose(0, 1, 3, 2)).astype(ml_dtypes.float8_e4m3fn).view(np.uint8)
    return words, np.ascontiguousarray(byte.astype(np.uint8).reshape(k // 512, 16, n))


def unpack_weight(words, scales):
    g, p, n, _ = words.shape
    vals = np.ascontiguousarray(words).view(ml_dtypes.float8_e4m3fn).astype(np.float64) * np.repeat(np.exp2(scales.astype(np.float64) - 127.0), 8, axis=1)[..., None]
    return vals.transpose(0, 1, 3, 2).reshape(g * 512, n)


K, T, S, N, G, H, W = 512, 2048, 512, 512, 2048, 512, 256


def setup_inputs():
    n = np.random.standard_normal
    s = mx_kscale(K)[:, None]
    u = mx_kscale(S)
    packed_xT = pack_weight(n((K, T)) * s)
    packed_dT = pack_weight(n((K, G)) / s)
    perm = np.random.permutation(S)
    return {
        "x_words": packed_xT[0],
        "x_scales": packed_xT[1],
        "d_words": packed_dT[0],
        "d_scales": packed_dT[1],
        "gn": (np.random.uniform(0.5, 1.5, (H, 1)) * u[:, None]).astype(np.float32),
        "w1": (n((H, N)) / np.sqrt(2 * H) / u[:, None]).astype(np.float32),
        "w2": (n((K, N)) / np.sqrt(2 * K) / s).astype(np.float32),
        "offs": striped(np.random.permutation(T)[:S]),
        "k1": striped8(np.random.randint(0, G, (8, H))),
        "n1": striped(np.random.randint(0, S, G)),
        "two": striped(np.random.permutation(T)[:S]),
        "n2": striped(perm[:W]),
        "n3": striped(perm[W:]),
    }


def reference(x_words, x_scales, d_words, d_scales, gn, w1, w2, offs, k1, n1, two, n2, n3):
    d_k1 = unpack_weight(d_words, d_scales)[np.arange(K)[:, None], runs(k1, K)]
    xq = unpack_weight(x_words, x_scales)[:, unstriped(offs)]
    s = 0.0625 * (d_k1.T @ xq)
    mb = s[:, unstriped(n1)]
    mx = mb.reshape(H, S, 4).max(axis=2)
    mn = mb.reshape(H, S, 4).min(axis=2)
    z = f64(gn) * (np.maximum(np.minimum(1.5 * s, mx), mn))
    x_two = unpack_weight(x_words, x_scales)[:, unstriped(two)]
    h = mxq(f64(w1), 0, "e4m3").T @ mxq(z, 0, "e4m3") + mxq(f64(w2), 0, "e4m3").T @ x_two
    pb = h[:, unstriped(n3)]
    pa = h[:, unstriped(n2)]
    rb = pb - (0.5 * pa)
    ra = np.sqrt((pa) ** 2 + (pb) ** 2 + 0.25)
    ds = np.zeros((N, S))
    ds[:, unstriped(n2)] = ra
    out = ds.copy()
    out[:, unstriped(n3)] = rb
    return out

@@ -1,0 +1,242 @@
+from contextlib import ExitStack
+
+import concourse.mybir as mybir
+
+K, T, S, N, G, H, W = 512, 2048, 512, 512, 2048, 512, 256
+FLOPS = 3 * 2 * 512 * 512 * 512
+
+F32 = mybir.dt.float32
+BF16 = mybir.dt.bfloat16
+I32 = mybir.dt.int32
+U32 = mybir.dt.uint32
+U16 = mybir.dt.uint16
+U8 = mybir.dt.uint8
+FP8X4 = mybir.dt.float8_e4m3fn_x4
+ALU = mybir.AluOpType
+ACT = mybir.ActivationFunctionType
+
+P = 128
+PACK = 4
+MEMBERS = 4
+HALF = S // 2
+PIECE = 512
+SPARE = 32
+
+
+def tile_picked_kmixgclippolar_none_p_kernel(
+    tc, x_words, x_scales, d_words, d_scales, gn, w1, w2, offs, k1, n1, two, n2, n3, out
+):
+    nc = tc.nc
+    with ExitStack() as ctx:
+        lists = ctx.enter_context(tc.tile_pool(name="lists", bufs=1))
+        keep = ctx.enter_context(tc.tile_pool(name="keep", bufs=1))
+        psum = ctx.enter_context(tc.psum_pool(name="psum", bufs=1))
+
+        def load_list(name, src):
+            tile = lists.tile(list(src.shape), U16, name=name)
+            nc.sync.dma_start(tile[:], src)
+            return tile
+
+        def load_words(name, src):
+            tile = keep.tile([P, T], U32, name=name)
+            nc.sync.dma_start(tile[:].bitcast(I32), src[0].rearrange("p n t -> p (n t)").bitcast(I32))
+            return tile
+
+        def load_weight(name, src, tag):
+            tile = keep.tile([P, PACK, N], F32, name=name, tag=tag, align_bytes=64)
+            nc.sync.dma_start(tile[:], src.rearrange("(p j) n -> p j n", j=PACK))
+            return tile
+
+        d_byte_table = keep.tile([P, G], U8, name="d_byte_table")
+        x_byte_table = keep.tile([P, T], U8, name="x_byte_table")
+
+        k1_list = load_list("k1_list", k1)
+        d_rows = d_scales[0].bitcast(I32)
+        nc.sync.dma_start(d_byte_table[:].bitcast(I32), d_rows.unsqueeze(1).to_broadcast([16, 8, G // 4]))
+        d_word_table = load_words("d_word_table", d_words)
+        offs_list = load_list("offs_list", offs)
+        x_rows = x_scales[0].bitcast(I32)
+        for q in range(4):
+            nc.scalar.dma_start(
+                x_byte_table[:].bitcast(I32)[32 * q : 32 * q + 32, :],
+                x_rows[4 * q : 4 * q + 4, :].unsqueeze(0).to_broadcast([8, 4, T // 4]),
+            )
+        x_word_table = load_words("x_word_table", x_words)
+        gain = keep.tile([P, PACK], F32, name="gain")
+        nc.gpsimd.dma_start(gain[:], gn.rearrange("(p t) o -> p (t o)", t=PACK))
+        two_list = load_list("two_list", two)
+        n1_list = load_list("n1_list", n1)
+        n2_list = load_list("n2_list", n2)
+        n3_list = load_list("n3_list", n3)
+
+        gain16 = keep.tile([P, PACK], F32, name="gain16")
+        nc.scalar.activation(gain16[:], gain[:], ACT.Copy, scale=0.0625)
+
+        def gather(name, table, offsets, dtype):
+            tile = keep.tile([P, S], dtype, name=name, align_bytes=64)
+            nc.vector.tensor_copy(tile[:], table[:].indirect(offsets[:]))
+            return tile
+
+        def deal(name, picked, dtype):
+            tile = keep.tile([P, H], dtype, name=name, align_bytes=64)
+            nc.vector.tensor_copy(
+                tile[:].rearrange("p (t m) -> p t m", t=PACK), picked[:].rearrange("p (m t) -> p t m", t=PACK)
+            )
+            return tile
+
+        key_scales = deal("key_scales", gather("picked_key_bytes", d_byte_table, k1_list, U8), U8)
+        for a in range(1, 4):
+            nc.scalar.dma_start(key_scales[:].bitcast(I32)[a:P:32, :], key_scales[:].bitcast(I32)[8 * a : P : 32, :])
+        w2_raw = load_weight("w2_raw", w2, "picked_key_bytes")
+        key_words = deal("key_words", gather("picked_key_words", d_word_table, k1_list, U32), U32)
+        w1_raw = load_weight("w1_raw", w1, "picked_key_words")
+        token_scales = gather("token_scales", x_byte_table, offs_list, U8)
+        token_words = gather("token_words", x_word_table, offs_list, U32)
+
+        scores = []
+        for t in range(PACK):
+            cols = slice(t * P, (t + 1) * P)
+            acc = psum.tile([P, S], F32, name=f"score_bank{t}")
+            nc.tensor.matmul_mx(
+                out=acc[:],
+                lhsT=key_words[:, cols].bitcast(FP8X4),
+                lhsT_scale=key_scales[:, cols],
+                rhs=token_words[:].bitcast(FP8X4),
+                rhs_scale=token_scales[:],
+                start=True,
+                stop=True,
+            )
+            window = keep.tile([P, S + SPARE], F32, name=f"scores{t}")
+            nc.gpsimd.memset(window[:, S:], 0.0)
+            nc.scalar.activation(window[:, :S], acc[:], ACT.Copy, scale=gain16[:, t : t + 1])
+            scores.append(window)
+
+        two_scales = gather("two_scales", x_byte_table, two_list, U8)
+        two_words = gather("two_words", x_word_table, two_list, U32)
+
+        def interleave_views(grouped, raw):
+            return (
+                grouped.rearrange("p (c i) t -> p c t i", i=4),
+                raw.rearrange("p t (c i) -> p c t i", i=4),
+            )
+
+        def quantize(grouped, codes, scales):
+            nc.vector.quantize_mx(out=codes.bitcast(FP8X4), scales=scales, in_=grouped.rearrange("p n t -> p (n t)"))
+
+        w2_grouped = keep.tile([P, N, PACK], BF16, name="w2_grouped", align_bytes=64)
+        w2_codes = keep.tile([P, N], U32, name="w2_codes", align_bytes=64)
+        w2_scales = keep.tile([P, N], U8, name="w2_scales", align_bytes=64)
+        nc.vector.tensor_copy(*interleave_views(w2_grouped[:], w2_raw[:]))
+        quantize(w2_grouped[:], w2_codes[:], w2_scales[:])
+
+        sums = []
+        for m in range(N // P):
+            cols = slice(m * P, (m + 1) * P)
+            acc = psum.tile([P, S], F32, name=f"sum_bank{m}")
+            nc.tensor.matmul_mx(
+                out=acc[:],
+                lhsT=w2_codes[:, cols].bitcast(FP8X4),
+                lhsT_scale=w2_scales[:, cols],
+                rhs=two_words[:].bitcast(FP8X4),
+                rhs_scale=two_scales[:],
+                start=True,
+                stop=False,
+            )
+            sums.append(acc)
+
+        z_codes = keep.tile([P, S], U32, name="z_codes", align_bytes=64)
+        z_scales = keep.tile([P, S], U8, name="z_scales", align_bytes=64)
+        for half in range(2):
+            cols = slice(half * HALF, (half + 1) * HALF)
+            capped = keep.tile([P, PACK, HALF], F32, name=f"capped{half}")
+            smallest = keep.tile([P, PACK, HALF], F32, name=f"smallest{half}")
+            for t in range(PACK):
+                members = keep.tile([P, HALF, MEMBERS], F32, name=f"members{half}{t}")
+                flat = members[:].rearrange("p j d -> p (j d)")
+                for u in range(HALF * MEMBERS // PIECE):
+                    first = (half * HALF * MEMBERS + u * PIECE) // 16
+                    nc.scalar.activation(
+                        flat[:, u * PIECE : (u + 1) * PIECE],
+                        scores[t][:].indirect(n1_list[:, first : first + PIECE // 16]),
+                        ACT.Copy,
+                    )
+                hi_pairs = keep.tile([P, HALF, 2], F32, name="hi_pairs")
+                lo_pairs = keep.tile([P, HALF, 2], F32, name="lo_pairs")
+                largest = keep.tile([P, HALF], F32, name="largest")
+                nc.vector.tensor_tensor(hi_pairs[:], members[:, :, 0:2], members[:, :, 2:4], ALU.max)
+                nc.vector.tensor_tensor(lo_pairs[:], members[:, :, 0:2], members[:, :, 2:4], ALU.min)
+                nc.vector.tensor_tensor(largest[:], hi_pairs[:, :, 0], hi_pairs[:, :, 1], ALU.max)
+                nc.vector.tensor_tensor(smallest[:, t, :], lo_pairs[:, :, 0], lo_pairs[:, :, 1], ALU.min)
+                nc.vector.scalar_tensor_tensor(
+                    capped[:, t, :], scores[t][:, cols], 1.5, largest[:], ALU.mult, ALU.min
+                )
+            z_grouped = keep.tile([P, HALF, PACK], BF16, name=f"z_grouped{half}", align_bytes=64)
+            z_view, capped_view = interleave_views(z_grouped[:], capped[:])
+            smallest_view = interleave_views(z_grouped[:], smallest[:])[1]
+            nc.vector.tensor_tensor(z_view, capped_view, smallest_view, ALU.max)
+            quantize(z_grouped[:], z_codes[:, cols], z_scales[:, cols])
+
+        w1_grouped = keep.tile([P, N, PACK], BF16, name="w1_grouped", align_bytes=64)
+        w1_codes = keep.tile([P, N], U32, name="w1_codes", align_bytes=64)
+        w1_scales = keep.tile([P, N], U8, name="w1_scales", align_bytes=64)
+        nc.scalar.copy(*interleave_views(w1_grouped[:], w1_raw[:]))
+        quantize(w1_grouped[:], w1_codes[:], w1_scales[:])
+
+        for m in range(N // P):
+            cols = slice(m * P, (m + 1) * P)
+            nc.tensor.matmul_mx(
+                out=sums[m][:],
+                lhsT=w1_codes[:, cols].bitcast(FP8X4),
+                lhsT_scale=w1_scales[:, cols],
+                rhs=z_codes[:].bitcast(FP8X4),
+                rhs_scale=z_scales[:],
+                start=False,
+                stop=True,
+            )
+
+        pairs = [keep.tile([P, 2 * W], F32, name=f"pair{m}") for m in range(N // P)]
+        squares = [keep.tile([P, 2 * W], F32, name=f"squares{m}") for m in range(N // P)]
+        radii = [keep.tile([P, W], F32, name=f"radius{m}") for m in range(N // P)]
+        results = [keep.tile([P, S], F32, name=f"result{m}") for m in range(N // P)]
+
+        def fetch(m):
+            h = keep.tile([P, S], F32, name=f"h{m}")
+            nc.vector.tensor_copy(h[:], sums[m][:])
+            nc.scalar.activation(pairs[m][:, :W], h[:].indirect(n2_list[:]), ACT.Copy, scale=-0.5)
+            nc.vector.tensor_copy(pairs[m][:, W:], h[:].indirect(n3_list[:]))
+            nc.scalar.activation(squares[m][:], pairs[m][:], ACT.Square)
+
+        def root(m):
+            radius2 = keep.tile([P, W], F32, name=f"radius2{m}")
+            nc.vector.scalar_tensor_tensor(radius2[:], squares[m][:, :W], 4.0, squares[m][:, W:], ALU.mult, ALU.add)
+            nc.scalar.activation(radii[m][:], radius2[:], ACT.Sqrt, bias=0.25)
+
+        def put_radius(m):
+            nc.scalar.activation(results[m][:].indirect(n2_list[:]), radii[m][:], ACT.Copy)
+
+        def put_difference(m):
+            nc.vector.tensor_tensor(results[m][:].indirect(n3_list[:]), pairs[m][:, :W], pairs[m][:, W:], ALU.add)
+
+        def store(m):
+            nc.sync.dma_start(out[m * P : (m + 1) * P, :], results[m][:])
+
+        fetch(0)
+        fetch(1)
+        root(0)
+        put_radius(0)
+        root(1)
+        put_difference(1)
+        fetch(2)
+        put_radius(1)
+        store(1)
+        fetch(3)
+        put_difference(0)
+        store(0)
+        root(2)
+        put_radius(2)
+        root(3)
+        put_difference(3)
+        put_difference(2)
+        store(2)
+        put_radius(3)
+        store(3)

@@ -19,8 +19,8 @@ P = 128
 PACK = 4
 MEMBERS = 4
 HALF = S // 2
-PIECE = 512
-SPARE = 32
+PIECE = 1024
+SPARE = 544
 
 
 def tile_picked_kmixgclippolar_none_p_kernel(
@@ -38,7 +38,7 @@ def tile_picked_kmixgclippolar_none_p_kernel(
             return tile
 
         def load_words(name, src):
-            tile = keep.tile([P, T], U32, name=name)
+            tile = keep.tile([P, T], U32, name=name, align_bytes=64)
             nc.sync.dma_start(tile[:].bitcast(I32), src[0].rearrange("p n t -> p (n t)").bitcast(I32))
             return tile
 
@@ -50,14 +50,18 @@ def tile_picked_kmixgclippolar_none_p_kernel(
         d_byte_table = keep.tile([P, G], U8, name="d_byte_table")
         x_byte_table = keep.tile([P, T], U8, name="x_byte_table")
 
-        k1_list = load_list("k1_list", k1)
+        warm = keep.tile([P, 2], F32, name="warm")
+        nc.vector.memset(warm[:, 0:1], 1.0)
+        nc.scalar.activation(warm[:, 1:2], warm[:, 0:1], ACT.Sqrt)
+
         d_rows = d_scales[0].bitcast(I32)
         nc.sync.dma_start(d_byte_table[:].bitcast(I32), d_rows.unsqueeze(1).to_broadcast([16, 8, G // 4]))
+        k1_list = load_list("k1_list", k1)
         d_word_table = load_words("d_word_table", d_words)
         offs_list = load_list("offs_list", offs)
         x_rows = x_scales[0].bitcast(I32)
         for q in range(4):
-            nc.scalar.dma_start(
+            nc.sync.dma_start(
                 x_byte_table[:].bitcast(I32)[32 * q : 32 * q + 32, :],
                 x_rows[4 * q : 4 * q + 4, :].unsqueeze(0).to_broadcast([8, 4, T // 4]),
             )
@@ -72,8 +76,8 @@ def tile_picked_kmixgclippolar_none_p_kernel(
         gain16 = keep.tile([P, PACK], F32, name="gain16")
         nc.scalar.activation(gain16[:], gain[:], ACT.Copy, scale=0.0625)
 
-        def gather(name, table, offsets, dtype):
-            tile = keep.tile([P, S], dtype, name=name, align_bytes=64)
+        def gather(name, table, offsets, dtype, tag=None):
+            tile = keep.tile([P, S], dtype, name=name, tag=tag or name, align_bytes=64)
             nc.vector.tensor_copy(tile[:], table[:].indirect(offsets[:]))
             return tile
 
@@ -87,11 +91,13 @@ def tile_picked_kmixgclippolar_none_p_kernel(
         key_scales = deal("key_scales", gather("picked_key_bytes", d_byte_table, k1_list, U8), U8)
         for a in range(1, 4):
             nc.scalar.dma_start(key_scales[:].bitcast(I32)[a:P:32, :], key_scales[:].bitcast(I32)[8 * a : P : 32, :])
-        w2_raw = load_weight("w2_raw", w2, "picked_key_bytes")
         key_words = deal("key_words", gather("picked_key_words", d_word_table, k1_list, U32), U32)
+        w2_raw = load_weight("w2_raw", w2, "d_word_table")
         w1_raw = load_weight("w1_raw", w1, "picked_key_words")
         token_scales = gather("token_scales", x_byte_table, offs_list, U8)
         token_words = gather("token_words", x_word_table, offs_list, U32)
+
+        two_words = gather("two_words", x_word_table, two_list, U32)
 
         scores = []
         for t in range(PACK):
@@ -108,11 +114,12 @@ def tile_picked_kmixgclippolar_none_p_kernel(
             )
             window = keep.tile([P, S + SPARE], F32, name=f"scores{t}")
             nc.gpsimd.memset(window[:, S:], 0.0)
-            nc.scalar.activation(window[:, :S], acc[:], ACT.Copy, scale=gain16[:, t : t + 1])
+            if t == 0:
+                nc.scalar.activation(window[:, :S], acc[:], ACT.Copy, scale=gain16[:, t : t + 1])
+            else:
+                nc.vector.tensor_scalar(window[:, :S], acc[:], gain16[:, t : t + 1], None, ALU.mult)
             scores.append(window)
-
-        two_scales = gather("two_scales", x_byte_table, two_list, U8)
-        two_words = gather("two_words", x_word_table, two_list, U32)
+        two_scales = gather("two_scales", x_byte_table, two_list, U8, tag="token_scales")
 
         def interleave_views(grouped, raw):
             return (
@@ -120,96 +127,112 @@ def tile_picked_kmixgclippolar_none_p_kernel(
                 raw.rearrange("p t (c i) -> p c t i", i=4),
             )
 
-        def quantize(grouped, codes, scales):
-            nc.vector.quantize_mx(out=codes.bitcast(FP8X4), scales=scales, in_=grouped.rearrange("p n t -> p (n t)"))
-
-        w2_grouped = keep.tile([P, N, PACK], BF16, name="w2_grouped", align_bytes=64)
-        w2_codes = keep.tile([P, N], U32, name="w2_codes", align_bytes=64)
-        w2_scales = keep.tile([P, N], U8, name="w2_scales", align_bytes=64)
-        nc.vector.tensor_copy(*interleave_views(w2_grouped[:], w2_raw[:]))
-        quantize(w2_grouped[:], w2_codes[:], w2_scales[:])
-
-        sums = []
-        for m in range(N // P):
-            cols = slice(m * P, (m + 1) * P)
-            acc = psum.tile([P, S], F32, name=f"sum_bank{m}")
-            nc.tensor.matmul_mx(
-                out=acc[:],
-                lhsT=w2_codes[:, cols].bitcast(FP8X4),
-                lhsT_scale=w2_scales[:, cols],
-                rhs=two_words[:].bitcast(FP8X4),
-                rhs_scale=two_scales[:],
-                start=True,
-                stop=False,
-            )
-            sums.append(acc)
-
-        z_codes = keep.tile([P, S], U32, name="z_codes", align_bytes=64)
-        z_scales = keep.tile([P, S], U8, name="z_scales", align_bytes=64)
-        for half in range(2):
-            cols = slice(half * HALF, (half + 1) * HALF)
-            capped = keep.tile([P, PACK, HALF], F32, name=f"capped{half}")
-            smallest = keep.tile([P, PACK, HALF], F32, name=f"smallest{half}")
-            for t in range(PACK):
-                members = keep.tile([P, HALF, MEMBERS], F32, name=f"members{half}{t}")
-                flat = members[:].rearrange("p j d -> p (j d)")
-                for u in range(HALF * MEMBERS // PIECE):
-                    first = (half * HALF * MEMBERS + u * PIECE) // 16
-                    nc.scalar.activation(
-                        flat[:, u * PIECE : (u + 1) * PIECE],
-                        scores[t][:].indirect(n1_list[:, first : first + PIECE // 16]),
-                        ACT.Copy,
-                    )
-                hi_pairs = keep.tile([P, HALF, 2], F32, name="hi_pairs")
-                lo_pairs = keep.tile([P, HALF, 2], F32, name="lo_pairs")
-                largest = keep.tile([P, HALF], F32, name="largest")
-                nc.vector.tensor_tensor(hi_pairs[:], members[:, :, 0:2], members[:, :, 2:4], ALU.max)
-                nc.vector.tensor_tensor(lo_pairs[:], members[:, :, 0:2], members[:, :, 2:4], ALU.min)
-                nc.vector.tensor_tensor(largest[:], hi_pairs[:, :, 0], hi_pairs[:, :, 1], ALU.max)
-                nc.vector.tensor_tensor(smallest[:, t, :], lo_pairs[:, :, 0], lo_pairs[:, :, 1], ALU.min)
-                nc.vector.scalar_tensor_tensor(
-                    capped[:, t, :], scores[t][:, cols], 1.5, largest[:], ALU.mult, ALU.min
+        def clip(half, t, capped, smallest):
+            members = keep.tile([P, HALF, MEMBERS], F32, name=f"members{half}{t}", align_bytes=64)
+            flat = members[:].rearrange("p j d -> p (j d)")
+            for u in range(HALF * MEMBERS // PIECE):
+                first = (half * HALF * MEMBERS + u * PIECE) // 16
+                nc.scalar.activation(
+                    flat[:, u * PIECE : (u + 1) * PIECE],
+                    scores[t][:].indirect(n1_list[:, first : first + PIECE // 16]),
+                    ACT.Copy,
                 )
-            z_grouped = keep.tile([P, HALF, PACK], BF16, name=f"z_grouped{half}", align_bytes=64)
-            z_view, capped_view = interleave_views(z_grouped[:], capped[:])
-            smallest_view = interleave_views(z_grouped[:], smallest[:])[1]
-            nc.vector.tensor_tensor(z_view, capped_view, smallest_view, ALU.max)
-            quantize(z_grouped[:], z_codes[:, cols], z_scales[:, cols])
-
-        w1_grouped = keep.tile([P, N, PACK], BF16, name="w1_grouped", align_bytes=64)
-        w1_codes = keep.tile([P, N], U32, name="w1_codes", align_bytes=64)
-        w1_scales = keep.tile([P, N], U8, name="w1_scales", align_bytes=64)
-        nc.scalar.copy(*interleave_views(w1_grouped[:], w1_raw[:]))
-        quantize(w1_grouped[:], w1_codes[:], w1_scales[:])
-
-        for m in range(N // P):
-            cols = slice(m * P, (m + 1) * P)
-            nc.tensor.matmul_mx(
-                out=sums[m][:],
-                lhsT=w1_codes[:, cols].bitcast(FP8X4),
-                lhsT_scale=w1_scales[:, cols],
-                rhs=z_codes[:].bitcast(FP8X4),
-                rhs_scale=z_scales[:],
-                start=False,
-                stop=True,
+            hi_pairs = keep.tile([P, HALF, 2], F32, name="hi_pairs")
+            lo_pairs = keep.tile([P, HALF, 2], F32, name="lo_pairs")
+            largest = keep.tile([P, HALF], F32, name="largest", align_bytes=64)
+            nc.vector.tensor_tensor(hi_pairs[:], members[:, :, 0:2], members[:, :, 2:4], ALU.max)
+            nc.vector.tensor_tensor(lo_pairs[:], members[:, :, 0:2], members[:, :, 2:4], ALU.min)
+            nc.vector.tensor_tensor(largest[:], hi_pairs[:, :, 0], hi_pairs[:, :, 1], ALU.max)
+            nc.vector.tensor_tensor(smallest[:, t, :], lo_pairs[:, :, 0], lo_pairs[:, :, 1], ALU.min)
+            nc.vector.scalar_tensor_tensor(
+                capped[:, t, :], scores[t][:, half * HALF : (half + 1) * HALF], 1.5, largest[:], ALU.mult, ALU.min
             )
+
+        def quantize(name, grouped, tag):
+            width = grouped.shape[1]
+            codes = keep.tile([P, width], U32, name=f"{name}_codes", tag=tag, align_bytes=64)
+            scales = keep.tile([P, width], U8, name=f"{name}_scales", align_bytes=64)
+            nc.vector.quantize_mx(
+                out=codes[:].bitcast(FP8X4), scales=scales[:], in_=grouped[:].rearrange("p n t -> p (n t)")
+            )
+            return codes, scales
+
+        def round_z(half, capped, smallest):
+            grouped = keep.tile([P, HALF, PACK], BF16, name=f"z_grouped{half}", align_bytes=64)
+            z_view, capped_view = interleave_views(grouped[:], capped[:])
+            nc.vector.tensor_tensor(z_view, capped_view, interleave_views(grouped[:], smallest[:])[1], ALU.max)
+            return grouped
+
+        def round_weight(name, raw, half):
+            grouped = keep.tile([P, HALF, PACK], BF16, name=name, align_bytes=64)
+            nc.scalar.copy(*interleave_views(grouped[:], raw[:, :, half * HALF : (half + 1) * HALF]))
+            return grouped
+
+        capped = [keep.tile([P, PACK, HALF], F32, name=f"capped{half}", align_bytes=64) for half in range(2)]
+        smallest = [keep.tile([P, PACK, HALF], F32, name=f"smallest{half}", align_bytes=64) for half in range(2)]
+        for t in range(PACK):
+            clip(0, t, capped[0], smallest[0])
+        z0_grouped = round_z(0, capped[0], smallest[0])
+        clip(1, 0, capped[1], smallest[1])
+        z_low = quantize("z0", z0_grouped, "z0_codes")
+        for t in range(1, PACK):
+            clip(1, t, capped[1], smallest[1])
+
+        sums = [psum.tile([P, S], F32, name=f"sum_bank{m}") for m in range(N // P)]
+
+        def add_pass(m, weight, moving, cols, start, stop):
+            own = slice(m % 2 * P, (m % 2 + 1) * P)
+            nc.tensor.matmul_mx(
+                out=sums[m][:, cols],
+                lhsT=weight[0][:, own].bitcast(FP8X4),
+                lhsT_scale=weight[1][:, own],
+                rhs=moving[0][:].bitcast(FP8X4),
+                rhs_scale=moving[1][:],
+                start=start,
+                stop=stop,
+            )
+
+        w2_grouped = round_weight("w2_grouped0", w2_raw, 0)
+        w1_grouped = round_weight("w1_grouped0", w1_raw, 0)
+        w2_first = quantize("w2_0", w2_grouped, "members13")
+        z1_grouped = round_z(1, capped[1], smallest[1])
+        w1_first = quantize("w1_0", w1_grouped, "largest")
+        z_high = quantize("z1", z1_grouped, "z1_codes")
+        for m in range(2):
+            add_pass(m, w2_first, (two_words, two_scales), slice(0, S), True, False)
+        for m in range(2):
+            add_pass(m, w1_first, z_low, slice(0, HALF), False, False)
+            add_pass(m, w1_first, z_high, slice(HALF, S), False, True)
+        w2_second = quantize("w2_1", round_weight("w2_grouped1", w2_raw, 1), "capped1")
+        w1_second = quantize("w1_1", round_weight("w1_grouped1", w1_raw, 1), "smallest1")
+        for m in range(2, 4):
+            add_pass(m, w2_second, (two_words, two_scales), slice(0, S), True, False)
+            add_pass(m, w1_second, z_low, slice(0, HALF), False, False)
+            add_pass(m, w1_second, z_high, slice(HALF, S), False, True)
 
         pairs = [keep.tile([P, 2 * W], F32, name=f"pair{m}") for m in range(N // P)]
         squares = [keep.tile([P, 2 * W], F32, name=f"squares{m}") for m in range(N // P)]
         radii = [keep.tile([P, W], F32, name=f"radius{m}") for m in range(N // P)]
         results = [keep.tile([P, S], F32, name=f"result{m}") for m in range(N // P)]
 
+        h_rows = [keep.tile([P, S], F32, name=f"h{m}") for m in range(N // P)]
+        radii2 = [keep.tile([P, W], F32, name=f"radius2{m}") for m in range(N // P)]
+
+        def leave_psum(m):
+            nc.scalar.copy(h_rows[m][:], sums[m][:])
+
         def fetch(m):
-            h = keep.tile([P, S], F32, name=f"h{m}")
-            nc.vector.tensor_copy(h[:], sums[m][:])
-            nc.scalar.activation(pairs[m][:, :W], h[:].indirect(n2_list[:]), ACT.Copy, scale=-0.5)
-            nc.vector.tensor_copy(pairs[m][:, W:], h[:].indirect(n3_list[:]))
-            nc.scalar.activation(squares[m][:], pairs[m][:], ACT.Square)
+            nc.scalar.activation(pairs[m][:, :W], h_rows[m][:].indirect(n2_list[:]), ACT.Copy, scale=-0.5)
+            nc.vector.tensor_copy(pairs[m][:, W:], h_rows[m][:].indirect(n3_list[:]))
+
+        def square(m):
+            nc.vector.tensor_tensor(squares[m][:], pairs[m][:], pairs[m][:], ALU.mult)
+
+        def add_squares(m):
+            nc.vector.scalar_tensor_tensor(radii2[m][:], squares[m][:, :W], 4.0, squares[m][:, W:], ALU.mult, ALU.add)
 
         def root(m):
-            radius2 = keep.tile([P, W], F32, name=f"radius2{m}")
-            nc.vector.scalar_tensor_tensor(radius2[:], squares[m][:, :W], 4.0, squares[m][:, W:], ALU.mult, ALU.add)
-            nc.scalar.activation(radii[m][:], radius2[:], ACT.Sqrt, bias=0.25)
+            nc.scalar.activation(radii[m][:], radii2[m][:], ACT.Sqrt, bias=0.25)
 
         def put_radius(m):
             nc.scalar.activation(results[m][:].indirect(n2_list[:]), radii[m][:], ACT.Copy)
@@ -220,23 +243,20 @@ def tile_picked_kmixgclippolar_none_p_kernel(
         def store(m):
             nc.sync.dma_start(out[m * P : (m + 1) * P, :], results[m][:])
 
-        fetch(0)
-        fetch(1)
-        root(0)
-        put_radius(0)
-        root(1)
-        put_difference(1)
-        fetch(2)
-        put_radius(1)
-        store(1)
-        fetch(3)
-        put_difference(0)
-        store(0)
-        root(2)
-        put_radius(2)
-        root(3)
-        put_difference(3)
-        put_difference(2)
-        store(2)
-        put_radius(3)
-        store(3)
+        def each(tiles, *steps):
+            for step in steps:
+                for m in tiles:
+                    step(m)
+
+        first, second = (0, 1), (2, 3)
+        each(first, leave_psum, fetch)
+        each(second, leave_psum)
+        each(first, square, add_squares, root)
+        each(second, fetch)
+        each(first, put_radius)
+        each(second, square, add_squares, root, put_difference)
+        for a, b in zip(first, second):
+            put_radius(b)
+            store(b)
+            put_difference(a)
+            store(a)

@@ -50,31 +50,31 @@ def tile_picked_kmixgclippolar_none_p_kernel(
         d_byte_table = keep.tile([P, G], U8, name="d_byte_table")
         x_byte_table = keep.tile([P, T], U8, name="x_byte_table")
 
+        gain = keep.tile([P, PACK], F32, name="gain")
+        nc.gpsimd.dma_start(gain[:], gn.rearrange("(p t) o -> p (t o)", t=PACK))
+        nc.vector.memset(d_byte_table[:].bitcast(I32), 0)
+        nc.vector.memset(x_byte_table[:].bitcast(I32), 0)
         warm = keep.tile([P, 2], F32, name="warm")
         nc.vector.memset(warm[:, 0:1], 1.0)
         nc.scalar.activation(warm[:, 1:2], warm[:, 0:1], ACT.Sqrt)
 
         d_rows = d_scales[0].bitcast(I32)
-        nc.sync.dma_start(d_byte_table[:].bitcast(I32), d_rows.unsqueeze(1).to_broadcast([16, 8, G // 4]))
         k1_list = load_list("k1_list", k1)
-        d_word_table = load_words("d_word_table", d_words)
+        for e in range(2):
+            nc.sync.dma_start(d_byte_table[:].bitcast(I32)[e:P:16, :], d_rows[e:16:2, :])
         offs_list = load_list("offs_list", offs)
+        d_word_table = load_words("d_word_table", d_words)
         x_rows = x_scales[0].bitcast(I32)
         for q in range(4):
-            nc.sync.dma_start(
-                x_byte_table[:].bitcast(I32)[32 * q : 32 * q + 32, :],
-                x_rows[4 * q : 4 * q + 4, :].unsqueeze(0).to_broadcast([8, 4, T // 4]),
-            )
+            nc.scalar.dma_start(x_byte_table[:].bitcast(I32)[32 * q : 32 * q + 4, :], x_rows[4 * q : 4 * q + 4, :])
         x_word_table = load_words("x_word_table", x_words)
-        gain = keep.tile([P, PACK], F32, name="gain")
-        nc.gpsimd.dma_start(gain[:], gn.rearrange("(p t) o -> p (t o)", t=PACK))
         two_list = load_list("two_list", two)
         n1_list = load_list("n1_list", n1)
         n2_list = load_list("n2_list", n2)
         n3_list = load_list("n3_list", n3)
 
         gain16 = keep.tile([P, PACK], F32, name="gain16")
-        nc.scalar.activation(gain16[:], gain[:], ACT.Copy, scale=0.0625)
+        nc.gpsimd.tensor_scalar(gain16[:], gain[:], 0.0625, 0.0, ALU.mult, ALU.add)
 
         def gather(name, table, offsets, dtype, tag=None):
             tile = keep.tile([P, S], dtype, name=name, tag=tag or name, align_bytes=64)
@@ -88,13 +88,15 @@ def tile_picked_kmixgclippolar_none_p_kernel(
             )
             return tile
 
-        key_scales = deal("key_scales", gather("picked_key_bytes", d_byte_table, k1_list, U8), U8)
-        for a in range(1, 4):
-            nc.scalar.dma_start(key_scales[:].bitcast(I32)[a:P:32, :], key_scales[:].bitcast(I32)[8 * a : P : 32, :])
+        key_bytes = deal("key_bytes", gather("picked_key_bytes", d_byte_table, k1_list, U8), U8)
+        key_scales = keep.tile([P, H], U8, name="key_scales", align_bytes=64)
+        nc.vector.tensor_copy(key_scales[:].bitcast(I32), key_bytes[:].bitcast(I32))
+        for e in range(2):
+            nc.scalar.dma_start(key_scales[:].bitcast(I32)[2 + e : P : 32, :], key_bytes[:].bitcast(I32)[16 + e : P : 32, :])
+        token_scales = gather("token_scales", x_byte_table, offs_list, U8)
         key_words = deal("key_words", gather("picked_key_words", d_word_table, k1_list, U32), U32)
         w2_raw = load_weight("w2_raw", w2, "d_word_table")
         w1_raw = load_weight("w1_raw", w1, "picked_key_words")
-        token_scales = gather("token_scales", x_byte_table, offs_list, U8)
         token_words = gather("token_words", x_word_table, offs_list, U32)
 
         two_words = gather("two_words", x_word_table, two_list, U32)

@@ -125,8 +125,8 @@ def tile_picked_kmixgclippolar_none_p_kernel(
 
         def interleave_views(grouped, raw):
             return (
-                grouped.rearrange("p (c i) t -> p c t i", i=4),
-                raw.rearrange("p t (c i) -> p c t i", i=4),
+                grouped.rearrange("p (c i) t -> p c t i", i=2),
+                raw.rearrange("p t (c i) -> p c t i", i=2),
             )
 
         def clip(half, t, capped, smallest):

from contextlib import ExitStack

import concourse.mybir as mybir

K, T, S, N, G, H, W = 512, 2048, 512, 512, 2048, 512, 256
FLOPS = 3 * 2 * 512 * 512 * 512

F32 = mybir.dt.float32
BF16 = mybir.dt.bfloat16
I32 = mybir.dt.int32
U32 = mybir.dt.uint32
U16 = mybir.dt.uint16
U8 = mybir.dt.uint8
FP8X4 = mybir.dt.float8_e4m3fn_x4
ALU = mybir.AluOpType
ACT = mybir.ActivationFunctionType

P = 128
PACK = 4
MEMBERS = 4
HALF = S // 2
PIECE = 1024
SPARE = 544


def tile_picked_kmixgclippolar_none_p_kernel(
    tc, x_words, x_scales, d_words, d_scales, gn, w1, w2, offs, k1, n1, two, n2, n3, out
):
    nc = tc.nc
    with ExitStack() as ctx:
        lists = ctx.enter_context(tc.tile_pool(name="lists", bufs=1))
        keep = ctx.enter_context(tc.tile_pool(name="keep", bufs=1))
        psum = ctx.enter_context(tc.psum_pool(name="psum", bufs=1))

        def load_list(name, src):
            tile = lists.tile(list(src.shape), U16, name=name)
            nc.sync.dma_start(tile[:], src)
            return tile

        def load_words(name, src):
            tile = keep.tile([P, T], U32, name=name, align_bytes=64)
            nc.sync.dma_start(tile[:].bitcast(I32), src[0].rearrange("p n t -> p (n t)").bitcast(I32))
            return tile

        def load_weight(name, src, tag):
            tile = keep.tile([P, PACK, N], F32, name=name, tag=tag, align_bytes=64)
            nc.sync.dma_start(tile[:], src.rearrange("(p j) n -> p j n", j=PACK))
            return tile

        d_byte_table = keep.tile([P, G], U8, name="d_byte_table")
        x_byte_table = keep.tile([P, T], U8, name="x_byte_table")

        gain = keep.tile([P, PACK], F32, name="gain")
        nc.gpsimd.dma_start(gain[:], gn.rearrange("(p t) o -> p (t o)", t=PACK))
        nc.vector.memset(d_byte_table[:].bitcast(I32), 0)
        nc.vector.memset(x_byte_table[:].bitcast(I32), 0)
        warm = keep.tile([P, 2], F32, name="warm")
        nc.vector.memset(warm[:, 0:1], 1.0)
        nc.scalar.activation(warm[:, 1:2], warm[:, 0:1], ACT.Sqrt)

        d_rows = d_scales[0].bitcast(I32)
        k1_list = load_list("k1_list", k1)
        for e in range(2):
            nc.sync.dma_start(d_byte_table[:].bitcast(I32)[e:P:16, :], d_rows[e:16:2, :])
        offs_list = load_list("offs_list", offs)
        d_word_table = load_words("d_word_table", d_words)
        x_rows = x_scales[0].bitcast(I32)
        for q in range(4):
            nc.scalar.dma_start(x_byte_table[:].bitcast(I32)[32 * q : 32 * q + 4, :], x_rows[4 * q : 4 * q + 4, :])
        x_word_table = load_words("x_word_table", x_words)
        two_list = load_list("two_list", two)
        n1_list = load_list("n1_list", n1)
        n2_list = load_list("n2_list", n2)
        n3_list = load_list("n3_list", n3)

        gain16 = keep.tile([P, PACK], F32, name="gain16")
        nc.gpsimd.tensor_scalar(gain16[:], gain[:], 0.0625, 0.0, ALU.mult, ALU.add)

        def gather(name, table, offsets, dtype, tag=None):
            tile = keep.tile([P, S], dtype, name=name, tag=tag or name, align_bytes=64)
            nc.vector.tensor_copy(tile[:], table[:].indirect(offsets[:]))
            return tile

        def deal(name, picked, dtype):
            tile = keep.tile([P, H], dtype, name=name, align_bytes=64)
            nc.vector.tensor_copy(
                tile[:].rearrange("p (t m) -> p t m", t=PACK), picked[:].rearrange("p (m t) -> p t m", t=PACK)
            )
            return tile

        key_bytes = deal("key_bytes", gather("picked_key_bytes", d_byte_table, k1_list, U8), U8)
        key_scales = keep.tile([P, H], U8, name="key_scales", align_bytes=64)
        nc.vector.tensor_copy(key_scales[:].bitcast(I32), key_bytes[:].bitcast(I32))
        for e in range(2):
            nc.scalar.dma_start(key_scales[:].bitcast(I32)[2 + e : P : 32, :], key_bytes[:].bitcast(I32)[16 + e : P : 32, :])
        token_scales = gather("token_scales", x_byte_table, offs_list, U8)
        key_words = deal("key_words", gather("picked_key_words", d_word_table, k1_list, U32), U32)
        w2_raw = load_weight("w2_raw", w2, "d_word_table")
        w1_raw = load_weight("w1_raw", w1, "picked_key_words")
        token_words = gather("token_words", x_word_table, offs_list, U32)

        two_words = gather("two_words", x_word_table, two_list, U32)

        scores = []
        for t in range(PACK):
            cols = slice(t * P, (t + 1) * P)
            acc = psum.tile([P, S], F32, name=f"score_bank{t}")
            nc.tensor.matmul_mx(
                out=acc[:],
                lhsT=key_words[:, cols].bitcast(FP8X4),
                lhsT_scale=key_scales[:, cols],
                rhs=token_words[:].bitcast(FP8X4),
                rhs_scale=token_scales[:],
                start=True,
                stop=True,
            )
            window = keep.tile([P, S + SPARE], F32, name=f"scores{t}")
            nc.gpsimd.memset(window[:, S:], 0.0)
            if t == 0:
                nc.scalar.activation(window[:, :S], acc[:], ACT.Copy, scale=gain16[:, t : t + 1])
            else:
                nc.vector.tensor_scalar(window[:, :S], acc[:], gain16[:, t : t + 1], None, ALU.mult)
            scores.append(window)
        two_scales = gather("two_scales", x_byte_table, two_list, U8, tag="token_scales")

        def interleave_views(grouped, raw):
            return (
                grouped.rearrange("p (c i) t -> p c t i", i=2),
                raw.rearrange("p t (c i) -> p c t i", i=2),
            )

        def clip(half, t, capped, smallest):
            members = keep.tile([P, HALF, MEMBERS], F32, name=f"members{half}{t}", align_bytes=64)
            flat = members[:].rearrange("p j d -> p (j d)")
            for u in range(HALF * MEMBERS // PIECE):
                first = (half * HALF * MEMBERS + u * PIECE) // 16
                nc.scalar.activation(
                    flat[:, u * PIECE : (u + 1) * PIECE],
                    scores[t][:].indirect(n1_list[:, first : first + PIECE // 16]),
                    ACT.Copy,
                )
            hi_pairs = keep.tile([P, HALF, 2], F32, name="hi_pairs")
            lo_pairs = keep.tile([P, HALF, 2], F32, name="lo_pairs")
            largest = keep.tile([P, HALF], F32, name="largest", align_bytes=64)
            nc.vector.tensor_tensor(hi_pairs[:], members[:, :, 0:2], members[:, :, 2:4], ALU.max)
            nc.vector.tensor_tensor(lo_pairs[:], members[:, :, 0:2], members[:, :, 2:4], ALU.min)
            nc.vector.tensor_tensor(largest[:], hi_pairs[:, :, 0], hi_pairs[:, :, 1], ALU.max)
            nc.vector.tensor_tensor(smallest[:, t, :], lo_pairs[:, :, 0], lo_pairs[:, :, 1], ALU.min)
            nc.vector.scalar_tensor_tensor(
                capped[:, t, :], scores[t][:, half * HALF : (half + 1) * HALF], 1.5, largest[:], ALU.mult, ALU.min
            )

        def quantize(name, grouped, tag):
            width = grouped.shape[1]
            codes = keep.tile([P, width], U32, name=f"{name}_codes", tag=tag, align_bytes=64)
            scales = keep.tile([P, width], U8, name=f"{name}_scales", align_bytes=64)
            nc.vector.quantize_mx(
                out=codes[:].bitcast(FP8X4), scales=scales[:], in_=grouped[:].rearrange("p n t -> p (n t)")
            )
            return codes, scales

        def round_z(half, capped, smallest):
            grouped = keep.tile([P, HALF, PACK], BF16, name=f"z_grouped{half}", align_bytes=64)
            z_view, capped_view = interleave_views(grouped[:], capped[:])
            nc.vector.tensor_tensor(z_view, capped_view, interleave_views(grouped[:], smallest[:])[1], ALU.max)
            return grouped

        def round_weight(name, raw, half):
            grouped = keep.tile([P, HALF, PACK], BF16, name=name, align_bytes=64)
            nc.scalar.copy(*interleave_views(grouped[:], raw[:, :, half * HALF : (half + 1) * HALF]))
            return grouped

        capped = [keep.tile([P, PACK, HALF], F32, name=f"capped{half}", align_bytes=64) for half in range(2)]
        smallest = [keep.tile([P, PACK, HALF], F32, name=f"smallest{half}", align_bytes=64) for half in range(2)]
        for t in range(PACK):
            clip(0, t, capped[0], smallest[0])
        z0_grouped = round_z(0, capped[0], smallest[0])
        clip(1, 0, capped[1], smallest[1])
        z_low = quantize("z0", z0_grouped, "z0_codes")
        for t in range(1, PACK):
            clip(1, t, capped[1], smallest[1])

        sums = [psum.tile([P, S], F32, name=f"sum_bank{m}") for m in range(N // P)]

        def add_pass(m, weight, moving, cols, start, stop):
            own = slice(m % 2 * P, (m % 2 + 1) * P)
            nc.tensor.matmul_mx(
                out=sums[m][:, cols],
                lhsT=weight[0][:, own].bitcast(FP8X4),
                lhsT_scale=weight[1][:, own],
                rhs=moving[0][:].bitcast(FP8X4),
                rhs_scale=moving[1][:],
                start=start,
                stop=stop,
            )

        w2_grouped = round_weight("w2_grouped0", w2_raw, 0)
        w1_grouped = round_weight("w1_grouped0", w1_raw, 0)
        w2_first = quantize("w2_0", w2_grouped, "members13")
        z1_grouped = round_z(1, capped[1], smallest[1])
        w1_first = quantize("w1_0", w1_grouped, "largest")
        z_high = quantize("z1", z1_grouped, "z1_codes")
        for m in range(2):
            add_pass(m, w2_first, (two_words, two_scales), slice(0, S), True, False)
        for m in range(2):
            add_pass(m, w1_first, z_low, slice(0, HALF), False, False)
            add_pass(m, w1_first, z_high, slice(HALF, S), False, True)
        w2_second = quantize("w2_1", round_weight("w2_grouped1", w2_raw, 1), "capped1")
        w1_second = quantize("w1_1", round_weight("w1_grouped1", w1_raw, 1), "smallest1")
        for m in range(2, 4):
            add_pass(m, w2_second, (two_words, two_scales), slice(0, S), True, False)
            add_pass(m, w1_second, z_low, slice(0, HALF), False, False)
            add_pass(m, w1_second, z_high, slice(HALF, S), False, True)

        pairs = [keep.tile([P, 2 * W], F32, name=f"pair{m}") for m in range(N // P)]
        squares = [keep.tile([P, 2 * W], F32, name=f"squares{m}") for m in range(N // P)]
        radii = [keep.tile([P, W], F32, name=f"radius{m}") for m in range(N // P)]
        results = [keep.tile([P, S], F32, name=f"result{m}") for m in range(N // P)]

        h_rows = [keep.tile([P, S], F32, name=f"h{m}") for m in range(N // P)]
        radii2 = [keep.tile([P, W], F32, name=f"radius2{m}") for m in range(N // P)]

        def leave_psum(m):
            nc.scalar.copy(h_rows[m][:], sums[m][:])

        def fetch(m):
            nc.scalar.activation(pairs[m][:, :W], h_rows[m][:].indirect(n2_list[:]), ACT.Copy, scale=-0.5)
            nc.vector.tensor_copy(pairs[m][:, W:], h_rows[m][:].indirect(n3_list[:]))

        def square(m):
            nc.vector.tensor_tensor(squares[m][:], pairs[m][:], pairs[m][:], ALU.mult)

        def add_squares(m):
            nc.vector.scalar_tensor_tensor(radii2[m][:], squares[m][:, :W], 4.0, squares[m][:, W:], ALU.mult, ALU.add)

        def root(m):
            nc.scalar.activation(radii[m][:], radii2[m][:], ACT.Sqrt, bias=0.25)

        def put_radius(m):
            nc.scalar.activation(results[m][:].indirect(n2_list[:]), radii[m][:], ACT.Copy)

        def put_difference(m):
            nc.vector.tensor_tensor(results[m][:].indirect(n3_list[:]), pairs[m][:, :W], pairs[m][:, W:], ALU.add)

        def store(m):
            nc.sync.dma_start(out[m * P : (m + 1) * P, :], results[m][:])

        def each(tiles, *steps):
            for step in steps:
                for m in tiles:
                    step(m)

        first, second = (0, 1), (2, 3)
        each(first, leave_psum, fetch)
        each(second, leave_psum)
        each(first, square, add_squares, root)
        each(second, fetch)
        each(first, put_radius)
        each(second, square, add_squares, root, put_difference)
        for a, b in zip(first, second):
            put_radius(b)
            store(b)
            put_difference(a)
            store(a)
